import numpy as np
import ml_dtypes


def mxq(x, axis, fmt="e4m3"):
    dtype, down = {"e4m3": (ml_dtypes.float8_e4m3fn, 7), "e5m2": (ml_dtypes.float8_e5m2, 14)}[fmt]
    v = np.moveaxis(np.asarray(x, np.float32).astype(ml_dtypes.bfloat16).astype(np.float64), axis, -1)
    blocks = v.reshape(v.shape[:-1] + (-1, 32))
    amax = np.abs(blocks).max(-1, keepdims=True)
    byte = np.maximum(np.where(amax > 0, np.frexp(amax)[1] - 1 + 127, 0) - down, 1)
    scale = np.exp2(byte - 127.0)
    codes = (blocks / scale).astype(np.float32).astype(dtype).astype(np.float64)
    return np.moveaxis((codes * scale).reshape(v.shape), -1, axis)


WIDE = False


def mx_kscale(k):
    if not WIDE:
        return np.ones(k)
    levels = np.array([10, -10, 5, -5, 0])
    if k % 512:
        return np.exp2(np.random.permutation(np.resize(levels, k // 32))).repeat(32)
    a = np.empty((k // 512, 16))
    for p in range(k // 512):
        a[p, :8] = np.random.permutation(np.resize(levels, 8))
        for g in range(8):
            far = levels[np.abs(levels - a[p, g]) >= 10]
            a[p, g + 8] = far[np.random.randint(len(far))]
    return np.exp2(a.ravel()).repeat(32)


def f64(x):
    return np.asarray(x).astype(np.float64)


def striped(idx):
    return np.tile(np.asarray(idx).reshape(-1, 16).T, (8, 1)).astype(np.uint16)


def unstriped(offs):
    return offs[:16].T.reshape(-1).astype(np.int64)


E2M1 = np.array([0.0, 0.5, 1.0, 1.5, 2.0, 3.0, 4.0, 6.0, -0.0, -0.5, -1.0, -1.5, -2.0, -3.0, -4.0, -6.0])


def pack_weight(w, fmt):
    k, n = w.shape
    w = f64(np.asarray(w, np.float32).astype(ml_dtypes.bfloat16)).reshape(k // 32, 32, n)
    amax = np.abs(w).max(1)
    if fmt == "e4m3":
        byte = np.frexp(amax)[1] - 1 + 127 - 7
    else:
        mant, ex = np.frexp(amax / 6.0)
        byte = np.where(mant > 0.5, ex, ex - 1) + 127
    byte = np.clip(np.where(amax > 0, byte, 1), 1, 254)
    scaled = (w * np.exp2(127.0 - byte)[:, None, :]).reshape(k, n).astype(np.float32)
    by_word = np.ascontiguousarray(scaled.reshape(k // 512, 128, 4, n).transpose(0, 1, 3, 2))
    if fmt == "e4m3":
        words = by_word.astype(ml_dtypes.float8_e4m3fn).view(np.uint8)
    else:
        c = by_word.astype(ml_dtypes.float4_e2m1fn).view(np.uint8) & 0xF
        words = (c[..., 0::2] | (c[..., 1::2] << 4)).reshape(k // 512, 128, 2 * n)
    return np.ascontiguousarray(words), np.ascontiguousarray(byte.astype(np.uint8).reshape(k // 512, 16, n))


def unpack_weight(words, scales, fmt):
    g, _, n = scales.shape
    words = np.ascontiguousarray(words).reshape(g, 128, n, -1)
    if fmt == "e4m3":
        vals = words.view(ml_dtypes.float8_e4m3fn).astype(np.float64)
    else:
        nib = np.empty((g, 128, n, 4), np.uint8)
        nib[..., 0::2] = words & 0xF
        nib[..., 1::2] = words >> 4
        vals = E2M1[nib]
    vals = vals * np.repeat(np.exp2(scales.astype(np.float64) - 127.0), 8, axis=1)[..., None]
    return vals.transpose(0, 1, 3, 2).reshape(g * 512, n)


def sigmoid(v):
    return 1.0 / (1.0 + np.exp(-v))


def bf(x):
    return np.asarray(x, np.float32).astype(ml_dtypes.bfloat16)


def planes(Y):
    r, m = Y.shape
    b = f64(bf(Y)).reshape(r // 32, 32, m)
    amax = np.abs(b).max(1)
    byte = np.clip(np.where(amax > 0, np.frexp(amax)[1] - 1 + 127 - 7, 1), 1, 254)
    codes = (b * np.exp2(127.0 - byte)[:, None, :]).reshape(r, m).astype(np.float32).astype(ml_dtypes.float8_e4m3fn).view(np.uint8)
    words = codes.reshape(r // 512, 128, 4, m).transpose(0, 1, 3, 2)
    return np.ascontiguousarray(words), np.ascontiguousarray(byte.astype(np.uint8).reshape(r // 512, 16, m))


K, R, F, T, J = 512, 512, 512, 2048, 512


def setup_inputs():
    n = np.random.standard_normal
    idx = np.random.permutation(T)[:J]
    fk = mx_kscale(K)
    ff = mx_kscale(F)
    tabp = pack_weight(n((K, T)) / fk[:, None], "e4m3")
    return {
        "tab_words": tabp[0],
        "tab_scales": tabp[1],
        "w1": (n((K, R)) * 1 / np.sqrt(K) * fk[:, None]).astype(np.float32),
        "gain": (np.random.uniform(0.5, 1.5, (R, 1))).astype(np.float32),
        "wo": (n((F, R)) * 1 / np.sqrt(F) * ff[:, None]).astype(np.float32),
        "dy": (n((F, J)) / ff[:, None]).astype(np.float32),
        "old": (0.5 * n((R, J))).astype(np.float32),
        "offs": striped(idx),
    }


def reference(tab_words, tab_scales, w1, gain, wo, dy, old, offs):
    idx = unstriped(offs)
    tabu = unpack_weight(tab_words, tab_scales, "e4m3")
    w1q = mxq(f64(w1), 0, "e4m3")
    tabidxg = tabu[:, idx]
    a = w1q.T @ tabidxg
    n1 = np.sqrt(np.mean(np.square(a), axis=1, keepdims=True) + 0.01)
    s = a / n1 * f64(gain)
    woq = mxq(f64(wo), 0, "e4m3")
    dyq = mxq(f64(dy), 0, "e4m3")
    c0 = woq.T @ dyq
    ds = c0 * sigmoid(s) + c0 * s * sigmoid(s) * (1.0 - sigmoid(s))
    dn1 = np.sum(ds * f64(gain) * a / np.square(n1) * (-1.0), axis=1, keepdims=True)
    da = ds * f64(gain) / n1 + dn1 * 0.5 / np.sqrt(np.mean(np.square(a), axis=1, keepdims=True) + 0.01) / 512.0 * a * 2.0
    y = da + f64(old)
    words, scales = planes(y)
    return y, words, scales

@@ -1,0 +1,175 @@
+from contextlib import ExitStack
+
+import concourse.mybir as mybir
+
+K, R, F, T, J = 512, 512, 512, 2048, 512
+FLOPS = 2 * K * R * J + 2 * F * R * J
+
+F32 = mybir.dt.float32
+BF16 = mybir.dt.bfloat16
+I32 = mybir.dt.int32
+U32 = mybir.dt.uint32
+U16 = mybir.dt.uint16
+U8 = mybir.dt.uint8
+FP8X4 = mybir.dt.float8_e4m3fn_x4
+ALU = mybir.AluOpType
+ACT = mybir.ActivationFunctionType
+
+P = 128
+PACK = 4
+HALF = 256
+EPS = 0.01
+
+
+def tile_attend_cslotnorm_pl_kernel(tc, tab_words, tab_scales, w1, gain, wo, dy, old, offs, out_0, out_1, out_2):
+    nc = tc.nc
+    with ExitStack() as ctx:
+        keep = ctx.enter_context(tc.tile_pool(name="keep", bufs=1))
+        psum = ctx.enter_context(tc.psum_pool(name="psum", bufs=1))
+
+        def sbuf(name, shape, dtype):
+            return keep.tile(shape, dtype, name=name, align_bytes=64)
+
+        offsets = keep.tile([P, J // 16], U16, name="offsets")
+        table_scales = sbuf("table_scales", [P, T], U8)
+        nc.vector.memset(table_scales[:].bitcast(I32), 0)
+        ones = sbuf("ones", [P, 1], F32)
+        nc.vector.memset(ones[:], 1.0)
+        root_inv_j = sbuf("root_inv_j", [P, 1], F32)
+        nc.scalar.activation(root_inv_j[:], ones[:], ACT.Sqrt, scale=1.0 / J)
+
+        w1_raw = sbuf("w1_raw", [P, PACK, R], F32)
+        nc.sync.dma_start(out=w1_raw[:], in_=w1.rearrange("(p i) r -> p i r", i=PACK))
+        for q in range(4):
+            nc.sync.dma_start(out=table_scales[32 * q : 32 * q + 4, :].bitcast(I32),
+                              in_=tab_scales[0, 4 * q : 4 * q + 4, :].bitcast(I32))
+        nc.sync.dma_start(offsets[:], offs)
+        table_words = sbuf("table_words", [P, T], I32)
+        nc.sync.dma_start(out=table_words[:], in_=tab_words[0].rearrange("p n t -> p (n t)").bitcast(I32))
+        gain_cols = sbuf("gain_cols", [P, PACK], F32)
+        nc.scalar.dma_start(out=gain_cols[:], in_=gain.rearrange("(p t) o -> p (t o)", t=PACK))
+        wo_raw, dy_raw, old_pair = [], [], []
+        for name, src, tiles in (("wo_raw", wo, wo_raw), ("dy_raw", dy, dy_raw)):
+            for u in range(2):
+                tiles.append(sbuf(f"{name}{u}", [P, PACK, HALF], F32))
+                nc.sync.dma_start(out=tiles[u][:],
+                                  in_=src.rearrange("(p i) c -> p i c", i=PACK)[:, :, u * HALF : (u + 1) * HALF])
+        for u in range(2):
+            old_pair.append(sbuf(f"old{u}", [P, 2, J], F32))
+            nc.sync.dma_start(out=old_pair[u][:], in_=old.rearrange("(p t) j -> p t j", t=PACK)[:, 2 * u : 2 * u + 2, :])
+
+        def quantise(name, grouped, width):
+            codes = sbuf(name + "_codes", [P, width], U32)
+            scales = sbuf(name + "_scales", [P, width], U8)
+            nc.vector.quantize_mx(out=codes[:].bitcast(FP8X4), scales=scales[:], in_=grouped[:])
+            return codes, scales
+
+        def dealt(grouped, u):
+            return grouped[:].rearrange("p (t m i) -> p m i t", t=PACK, i=PACK)[:, 64 * u : 64 * (u + 1), :, :]
+
+        w1_grouped = sbuf("w1_grouped", [P, PACK * R], BF16)
+        w1_view = w1_raw[:].rearrange("p i (m t) -> p m i t", t=PACK)
+        nc.scalar.copy(dealt(w1_grouped, 0), w1_view[:, 0:64, :, :])
+        nc.vector.tensor_copy(dealt(w1_grouped, 1), w1_view[:, 64:128, :, :])
+        picked_scales = sbuf("picked_scales", [P, J], U8)
+        nc.vector.tensor_copy(picked_scales[:], table_scales[:].indirect(offsets[:]))
+        w1_codes, w1_scales = quantise("w1", w1_grouped, R)
+        picked_words = []
+        for u in range(2):
+            picked_words.append(sbuf(f"picked_words{u}", [P, HALF], U32))
+            nc.vector.tensor_copy(picked_words[u][:],
+                                  table_words[:].bitcast(U32).indirect(offsets[:, 16 * u : 16 * (u + 1)]))
+        a_bank = [psum.tile([P, J], F32, name=f"a{t}") for t in range(PACK)]
+        for t in range(PACK):
+            for u in range(2):
+                cols = slice(u * HALF, (u + 1) * HALF)
+                nc.tensor.matmul_mx(out=a_bank[t][:, cols],
+                                    lhsT=w1_codes[:, t * P : (t + 1) * P].bitcast(FP8X4),
+                                    lhsT_scale=w1_scales[:, t * P : (t + 1) * P],
+                                    rhs=picked_words[u][:].bitcast(FP8X4),
+                                    rhs_scale=picked_scales[:, cols], start=True, stop=True)
+
+        neg_silu = [sbuf(f"neg_silu{t}", [P, J], F32) for t in range(PACK)]
+        neg_tanh = [sbuf(f"neg_tanh{t}", [P, J], F32) for t in range(PACK)]
+        mean_sq = sbuf("mean_sq", [P, PACK], F32)
+        for t in range(PACK):
+            nc.scalar.activation(neg_silu[t][:], a_bank[t][:], ACT.Square, scale=root_inv_j[:],
+                                 accum_out=mean_sq[:, t : t + 1])
+        norm = sbuf("norm", [P, PACK], F32)
+        nc.scalar.activation(norm[:], mean_sq[:], ACT.Sqrt, bias=EPS)
+
+        wo_grouped = sbuf("wo_grouped", [P, PACK * R], BF16)
+        for u in range(2):
+            nc.vector.tensor_copy(dealt(wo_grouped, u), wo_raw[u][:].rearrange("p i (m t) -> p m i t", t=PACK))
+        wo_codes, wo_scales = quantise("wo", wo_grouped, R)
+        dy_grouped = [sbuf(f"dy_grouped{u}", [P, PACK * HALF], BF16) for u in range(2)]
+        for u in range(2):
+            nc.vector.tensor_copy(dy_grouped[u][:].rearrange("p (c e i) -> p c i e", e=4, i=PACK),
+                                  dy_raw[u][:].rearrange("p i (c e) -> p c i e", e=4))
+        inv_norm = dy_raw[1][:, 0, 0:PACK]
+        nc.vector.reciprocal(inv_norm, norm[:])
+        dy_quant = [quantise("dy0", dy_grouped[0], HALF)]
+        neg_g = sbuf("neg_g", [P, PACK], F32)
+        neg_half_g = sbuf("neg_half_g", [P, PACK], F32)
+        inv_sq = sbuf("inv_sq", [P, PACK], F32)
+        coef = sbuf("coef", [P, PACK], F32)
+        nc.vector.scalar_tensor_tensor(neg_g[:], inv_norm, -1.0, gain_cols[:], ALU.mult, ALU.mult)
+        nc.vector.scalar_tensor_tensor(neg_half_g[:], inv_norm, -0.5, gain_cols[:], ALU.mult, ALU.mult)
+        dy_quant.append(quantise("dy1", dy_grouped[1], HALF))
+        nc.vector.scalar_tensor_tensor(inv_sq[:], inv_norm, 1.0 / J, inv_norm, ALU.mult, ALU.mult)
+        nc.vector.tensor_tensor(coef[:], inv_sq[:], neg_half_g[:], ALU.mult)
+        c_bank = [psum.tile([P, J], F32, name=f"c{t}") for t in range(PACK)]
+        for t in range(PACK):
+            for u in range(2):
+                nc.tensor.matmul_mx(out=c_bank[t][:, u * HALF : (u + 1) * HALF],
+                                    lhsT=wo_codes[:, t * P : (t + 1) * P].bitcast(FP8X4),
+                                    lhsT_scale=wo_scales[:, t * P : (t + 1) * P],
+                                    rhs=dy_quant[u][0][:].bitcast(FP8X4),
+                                    rhs_scale=dy_quant[u][1][:], start=True, stop=True)
+
+        part = [sbuf(f"part{t}", [P, J], F32) for t in range(PACK)]
+        two_ds = [sbuf(f"two_ds{t}", [P, J], F32) for t in range(PACK)]
+        inner = [sbuf(f"inner{t}", [P, J], F32) for t in range(PACK)]
+        row_coef = [sbuf(f"row_coef{t}", [P, 1], F32) for t in range(PACK)]
+        y_pair = [sbuf(f"y{u}", [P, 2, J], F32) for u in range(2)]
+        y_grouped = sbuf("y_grouped", [P, PACK * J], BF16)
+        y_words = y_grouped[:].rearrange("p (j t) -> p j t", t=PACK)
+        out_rows = out_0.rearrange("(p t) j -> p t j", t=PACK)
+        for u in range(2):
+            pair = (2 * u, 2 * u + 1)
+            for t in pair:
+                nc.scalar.activation(neg_silu[t][:], a_bank[t][:], ACT.Silu, scale=neg_g[:, t : t + 1])
+            for t in pair:
+                nc.scalar.activation(neg_tanh[t][:], a_bank[t][:], ACT.Tanh, scale=neg_half_g[:, t : t + 1])
+            for t in pair:
+                nc.vector.scalar_tensor_tensor(part[t][:], neg_silu[t][:], -1.0, c_bank[t][:], ALU.add, ALU.mult)
+            for t in pair:
+                nc.vector.scalar_tensor_tensor(two_ds[t][:], neg_tanh[t][:], -1.0, part[t][:], ALU.add, ALU.mult)
+            for t in pair:
+                nc.vector.scalar_tensor_tensor(part[t][:], two_ds[t][:], coef[:, t : t + 1], a_bank[t][:],
+                                               ALU.mult, ALU.mult, accum_out=row_coef[t][:])
+                nc.vector.scalar_tensor_tensor(inner[t][:], two_ds[t][:], neg_half_g[:, t : t + 1],
+                                               old_pair[u][:, t % 2, :], ALU.mult, ALU.subtract)
+            for t in pair:
+                nc.vector.scalar_tensor_tensor(y_pair[u][:, t % 2, :], a_bank[t][:], row_coef[t][:], inner[t][:],
+                                               ALU.mult, ALU.subtract)
+                nc.sync.dma_start(out=out_rows[:, t, :], in_=y_pair[u][:, t % 2, :])
+            y_turned = y_pair[u][:].rearrange("p e j -> p j e")
+            if u == 0:
+                nc.scalar.copy(y_words[:, :, 0:2], y_turned)
+            else:
+                nc.vector.tensor_copy(y_words[:, 0:HALF, 2:4], y_turned[:, 0:HALF, :])
+                nc.scalar.copy(y_words[:, HALF:J, 2:4], y_turned[:, HALF:J, :])
+
+        y_codes = sbuf("y_codes", [P, J], U32)
+        y_scales = sbuf("y_scales", [P, J], U8)
+        out_words = out_1[0].rearrange("p n t -> p (n t)").bitcast(I32)
+        for u in range(2):
+            cols = slice(u * HALF, (u + 1) * HALF)
+            nc.vector.quantize_mx(out=y_codes[:, cols].bitcast(FP8X4), scales=y_scales[:, cols],
+                                  in_=y_grouped[:, PACK * HALF * u : PACK * HALF * (u + 1)])
+            nc.sync.dma_start(out=out_words[:, cols], in_=y_codes[:, cols].bitcast(I32))
+        for q in range(4):
+            queue = nc.scalar if q % 2 == 0 else nc.sync
+            queue.dma_start(out=out_2[0, 4 * q : 4 * q + 4, :].bitcast(I32),
+                            in_=y_scales[32 * q : 32 * q + 4, :].bitcast(I32))

@@ -38,22 +38,25 @@ def tile_attend_cslotnorm_pl_kernel(tc, tab_words, tab_scales, w1, gain, wo, dy,
         root_inv_j = sbuf("root_inv_j", [P, 1], F32)
         nc.scalar.activation(root_inv_j[:], ones[:], ACT.Sqrt, scale=1.0 / J)
 
+        scale_rows = sbuf("scale_rows", [P, T // 4], I32)
+        for q in range(4):
+            queue = nc.scalar if q % 2 == 0 else nc.sync
+            queue.dma_start(out=scale_rows[q:P:32, :], in_=tab_scales[0, q:16:4, :].bitcast(I32))
+        for q in range(4):
+            rows = slice(32 * q, 32 * q + 4)
+            nc.vector.tensor_copy(table_scales[rows, :].bitcast(I32), scale_rows[rows, :])
         w1_raw = sbuf("w1_raw", [P, PACK, R], F32)
         nc.sync.dma_start(out=w1_raw[:], in_=w1.rearrange("(p i) r -> p i r", i=PACK))
-        for q in range(4):
-            nc.sync.dma_start(out=table_scales[32 * q : 32 * q + 4, :].bitcast(I32),
-                              in_=tab_scales[0, 4 * q : 4 * q + 4, :].bitcast(I32))
         nc.sync.dma_start(offsets[:], offs)
         table_words = sbuf("table_words", [P, T], I32)
         nc.sync.dma_start(out=table_words[:], in_=tab_words[0].rearrange("p n t -> p (n t)").bitcast(I32))
+        wo_raw = sbuf("wo_raw", [P, PACK, R], F32)
+        nc.sync.dma_start(out=wo_raw[:], in_=wo.rearrange("(p i) r -> p i r", i=PACK))
+        dy_raw = sbuf("dy_raw", [P, PACK, J], F32)
+        nc.sync.dma_start(out=dy_raw[:], in_=dy.rearrange("(p i) j -> p i j", i=PACK))
         gain_cols = sbuf("gain_cols", [P, PACK], F32)
-        nc.scalar.dma_start(out=gain_cols[:], in_=gain.rearrange("(p t) o -> p (t o)", t=PACK))
-        wo_raw, dy_raw, old_pair = [], [], []
-        for name, src, tiles in (("wo_raw", wo, wo_raw), ("dy_raw", dy, dy_raw)):
-            for u in range(2):
-                tiles.append(sbuf(f"{name}{u}", [P, PACK, HALF], F32))
-                nc.sync.dma_start(out=tiles[u][:],
-                                  in_=src.rearrange("(p i) c -> p i c", i=PACK)[:, :, u * HALF : (u + 1) * HALF])
+        nc.sync.dma_start(out=gain_cols[:], in_=gain.rearrange("(p t) o -> p (t o)", t=PACK))
+        old_pair = []
         for u in range(2):
             old_pair.append(sbuf(f"old{u}", [P, 2, J], F32))
             nc.sync.dma_start(out=old_pair[u][:], in_=old.rearrange("(p t) j -> p t j", t=PACK)[:, 2 * u : 2 * u + 2, :])
@@ -64,13 +67,13 @@ def tile_attend_cslotnorm_pl_kernel(tc, tab_words, tab_scales, w1, gain, wo, dy,
             nc.vector.quantize_mx(out=codes[:].bitcast(FP8X4), scales=scales[:], in_=grouped[:])
             return codes, scales
 
-        def dealt(grouped, u):
-            return grouped[:].rearrange("p (t m i) -> p m i t", t=PACK, i=PACK)[:, 64 * u : 64 * (u + 1), :, :]
+        def dealt(grouped):
+            return grouped[:].rearrange("p (t m i) -> p m i t", t=PACK, i=PACK)
 
         w1_grouped = sbuf("w1_grouped", [P, PACK * R], BF16)
         w1_view = w1_raw[:].rearrange("p i (m t) -> p m i t", t=PACK)
-        nc.scalar.copy(dealt(w1_grouped, 0), w1_view[:, 0:64, :, :])
-        nc.vector.tensor_copy(dealt(w1_grouped, 1), w1_view[:, 64:128, :, :])
+        nc.scalar.copy(dealt(w1_grouped)[:, 0:80, :, :], w1_view[:, 0:80, :, :])
+        nc.vector.tensor_copy(dealt(w1_grouped)[:, 80:128, :, :], w1_view[:, 80:128, :, :])
         picked_scales = sbuf("picked_scales", [P, J], U8)
         nc.vector.tensor_copy(picked_scales[:], table_scales[:].indirect(offsets[:]))
         w1_codes, w1_scales = quantise("w1", w1_grouped, R)
@@ -99,14 +102,14 @@ def tile_attend_cslotnorm_pl_kernel(tc, tab_words, tab_scales, w1, gain, wo, dy,
         nc.scalar.activation(norm[:], mean_sq[:], ACT.Sqrt, bias=EPS)
 
         wo_grouped = sbuf("wo_grouped", [P, PACK * R], BF16)
-        for u in range(2):
-            nc.vector.tensor_copy(dealt(wo_grouped, u), wo_raw[u][:].rearrange("p i (m t) -> p m i t", t=PACK))
+        nc.vector.tensor_copy(wo_grouped[:].rearrange("p (t m i) -> p m i t", t=PACK, i=PACK),
+                              wo_raw[:].rearrange("p i (m t) -> p m i t", t=PACK))
         wo_codes, wo_scales = quantise("wo", wo_grouped, R)
         dy_grouped = [sbuf(f"dy_grouped{u}", [P, PACK * HALF], BF16) for u in range(2)]
         for u in range(2):
             nc.vector.tensor_copy(dy_grouped[u][:].rearrange("p (c e i) -> p c i e", e=4, i=PACK),
-                                  dy_raw[u][:].rearrange("p i (c e) -> p c i e", e=4))
-        inv_norm = dy_raw[1][:, 0, 0:PACK]
+                                  dy_raw[:, :, u * HALF : (u + 1) * HALF].rearrange("p i (c e) -> p c i e", e=4))
+        inv_norm = dy_raw[:, 0, HALF : HALF + PACK]
         nc.vector.reciprocal(inv_norm, norm[:])
         dy_quant = [quantise("dy0", dy_grouped[0], HALF)]
         neg_g = sbuf("neg_g", [P, PACK], F32)
@@ -129,12 +132,16 @@ def tile_attend_cslotnorm_pl_kernel(tc, tab_words, tab_scales, w1, gain, wo, dy,
 
         part = [sbuf(f"part{t}", [P, J], F32) for t in range(PACK)]
         two_ds = [sbuf(f"two_ds{t}", [P, J], F32) for t in range(PACK)]
-        inner = [sbuf(f"inner{t}", [P, J], F32) for t in range(PACK)]
+        inner = [sbuf(f"inner{t}", [P, J], F32) if t != 1 else None for t in range(PACK)]
         row_coef = [sbuf(f"row_coef{t}", [P, 1], F32) for t in range(PACK)]
         y_pair = [sbuf(f"y{u}", [P, 2, J], F32) for u in range(2)]
         y_grouped = sbuf("y_grouped", [P, PACK * J], BF16)
         y_words = y_grouped[:].rearrange("p (j t) -> p j t", t=PACK)
         out_rows = out_0.rearrange("(p t) j -> p t j", t=PACK)
+
+        def old_rows(t):
+            return old_pair[t // 2][:, t % 2, :]
+
         for u in range(2):
             pair = (2 * u, 2 * u + 1)
             for t in pair:
@@ -145,21 +152,41 @@ def tile_attend_cslotnorm_pl_kernel(tc, tab_words, tab_scales, w1, gain, wo, dy,
                 nc.vector.scalar_tensor_tensor(part[t][:], neg_silu[t][:], -1.0, c_bank[t][:], ALU.add, ALU.mult)
             for t in pair:
                 nc.vector.scalar_tensor_tensor(two_ds[t][:], neg_tanh[t][:], -1.0, part[t][:], ALU.add, ALU.mult)
-            for t in pair:
-                nc.vector.scalar_tensor_tensor(part[t][:], two_ds[t][:], coef[:, t : t + 1], a_bank[t][:],
-                                               ALU.mult, ALU.mult, accum_out=row_coef[t][:])
-                nc.vector.scalar_tensor_tensor(inner[t][:], two_ds[t][:], neg_half_g[:, t : t + 1],
-                                               old_pair[u][:, t % 2, :], ALU.mult, ALU.subtract)
-            for t in pair:
-                nc.vector.scalar_tensor_tensor(y_pair[u][:, t % 2, :], a_bank[t][:], row_coef[t][:], inner[t][:],
-                                               ALU.mult, ALU.subtract)
-                nc.sync.dma_start(out=out_rows[:, t, :], in_=y_pair[u][:, t % 2, :])
-            y_turned = y_pair[u][:].rearrange("p e j -> p j e")
             if u == 0:
-                nc.scalar.copy(y_words[:, :, 0:2], y_turned)
-            else:
-                nc.vector.tensor_copy(y_words[:, 0:HALF, 2:4], y_turned[:, 0:HALF, :])
-                nc.scalar.copy(y_words[:, HALF:J, 2:4], y_turned[:, HALF:J, :])
+                nc.vector.scalar_tensor_tensor(inner[0][:], two_ds[0][:], neg_half_g[:, 0:1], old_rows(0),
+                                               ALU.mult, ALU.subtract)
+        inner[1] = neg_tanh[3]
+        for t in range(1, PACK):
+            nc.scalar.activation(neg_silu[t][:], two_ds[t][:], ACT.Copy, scale=neg_half_g[:, t : t + 1])
+            nc.gpsimd.tensor_tensor(inner[t][:], neg_silu[t][:], old_rows(t), ALU.subtract)
+
+        def row_sum(t):
+            nc.vector.scalar_tensor_tensor(part[t][:], two_ds[t][:], coef[:, t : t + 1], a_bank[t][:],
+                                           ALU.mult, ALU.mult, accum_out=row_coef[t][:])
+
+        def result(t, cols):
+            nc.vector.scalar_tensor_tensor(y_pair[t // 2][:, t % 2, cols], a_bank[t][:, cols], row_coef[t][:],
+                                           inner[t][:, cols], ALU.mult, ALU.subtract)
+
+        def store(t):
+            nc.sync.dma_start(out=out_rows[:, t, :], in_=y_pair[t // 2][:, t % 2, :])
+
+        for t in (0, 1):
+            row_sum(t)
+        for t in (0, 1):
+            result(t, slice(0, J))
+            store(t)
+        nc.scalar.copy(y_words[:, :, 0:2], y_pair[0][:].rearrange("p e j -> p j e"))
+        for t in (2, 3):
+            row_sum(t)
+        y_turned = y_pair[1][:].rearrange("p e j -> p j e")
+        for t in (2, 3):
+            result(t, slice(0, HALF))
+        nc.scalar.copy(y_words[:, 0:HALF, 2:4], y_turned[:, 0:HALF, :])
+        for t in (2, 3):
+            result(t, slice(HALF, J))
+            store(t)
+        nc.vector.tensor_copy(y_words[:, HALF:J, 2:4], y_turned[:, HALF:J, :])
 
         y_codes = sbuf("y_codes", [P, J], U32)
         y_scales = sbuf("y_scales", [P, J], U8)
@@ -171,5 +198,4 @@ def tile_attend_cslotnorm_pl_kernel(tc, tab_words, tab_scales, w1, gain, wo, dy,
             nc.sync.dma_start(out=out_words[:, cols], in_=y_codes[:, cols].bitcast(I32))
         for q in range(4):
             queue = nc.scalar if q % 2 == 0 else nc.sync
-            queue.dma_start(out=out_2[0, 4 * q : 4 * q + 4, :].bitcast(I32),
-                            in_=y_scales[32 * q : 32 * q + 4, :].bitcast(I32))
+            queue.dma_start(out=out_2[0, q:16:4, :].bitcast(I32), in_=y_scales[q:P:32, :].bitcast(I32))

@@ -27,16 +27,18 @@ def tile_attend_cslotnorm_pl_kernel(tc, tab_words, tab_scales, w1, gain, wo, dy,
         keep = ctx.enter_context(tc.tile_pool(name="keep", bufs=1))
         psum = ctx.enter_context(tc.psum_pool(name="psum", bufs=1))
 
-        def sbuf(name, shape, dtype):
-            return keep.tile(shape, dtype, name=name, align_bytes=64)
+        def sbuf(name, shape, dtype, tag=None):
+            return keep.tile(shape, dtype, name=name, tag=tag or name, align_bytes=64)
 
         offsets = keep.tile([P, J // 16], U16, name="offsets")
         table_scales = sbuf("table_scales", [P, T], U8)
         nc.vector.memset(table_scales[:].bitcast(I32), 0)
-        ones = sbuf("ones", [P, 1], F32)
-        nc.vector.memset(ones[:], 1.0)
-        root_inv_j = sbuf("root_inv_j", [P, 1], F32)
-        nc.scalar.activation(root_inv_j[:], ones[:], ACT.Sqrt, scale=1.0 / J)
+        zero = sbuf("zero", [P, 1], F32)
+        nc.vector.memset(zero[:], 0.0)
+        minus_half = sbuf("minus_half", [P, 2], F32)
+        nc.vector.memset(minus_half[:], -0.5)
+        zero_bias = sbuf("zero_bias", [P, 1], F32)
+        nc.scalar.activation(zero_bias[:], zero[:], ACT.Silu)
 
         scale_rows = sbuf("scale_rows", [P, T // 4], I32)
         for q in range(4):
@@ -48,14 +50,17 @@ def tile_attend_cslotnorm_pl_kernel(tc, tab_words, tab_scales, w1, gain, wo, dy,
         w1_raw = sbuf("w1_raw", [P, PACK, R], F32)
         nc.sync.dma_start(out=w1_raw[:], in_=w1.rearrange("(p i) r -> p i r", i=PACK))
         nc.sync.dma_start(offsets[:], offs)
+        gain_cols = sbuf("gain_cols", [P, PACK], F32)
+        nc.sync.dma_start(out=gain_cols[:], in_=gain.rearrange("(p t) o -> p (t o)", t=PACK))
+        neg_gains = sbuf("neg_gains", [P, PACK, 3], F32)
+        for column, factor in enumerate((-0.5, -1.0, -0.5)):
+            nc.vector.tensor_scalar(neg_gains[:, :, column], gain_cols[:], factor, None, ALU.mult)
         table_words = sbuf("table_words", [P, T], I32)
         nc.sync.dma_start(out=table_words[:], in_=tab_words[0].rearrange("p n t -> p (n t)").bitcast(I32))
         wo_raw = sbuf("wo_raw", [P, PACK, R], F32)
         nc.sync.dma_start(out=wo_raw[:], in_=wo.rearrange("(p i) r -> p i r", i=PACK))
         dy_raw = sbuf("dy_raw", [P, PACK, J], F32)
         nc.sync.dma_start(out=dy_raw[:], in_=dy.rearrange("(p i) j -> p i j", i=PACK))
-        gain_cols = sbuf("gain_cols", [P, PACK], F32)
-        nc.sync.dma_start(out=gain_cols[:], in_=gain.rearrange("(p t) o -> p (t o)", t=PACK))
         old_pair = []
         for u in range(2):
             old_pair.append(sbuf(f"old{u}", [P, 2, J], F32))
@@ -64,7 +69,7 @@ def tile_attend_cslotnorm_pl_kernel(tc, tab_words, tab_scales, w1, gain, wo, dy,
         def quantise(name, grouped, width):
             codes = sbuf(name + "_codes", [P, width], U32)
             scales = sbuf(name + "_scales", [P, width], U8)
-            nc.vector.quantize_mx(out=codes[:].bitcast(FP8X4), scales=scales[:], in_=grouped[:])
+            nc.vector.quantize_mx(out=codes[:].bitcast(FP8X4), scales=scales[:], in_=grouped)
             return codes, scales
 
         def dealt(grouped):
@@ -76,7 +81,7 @@ def tile_attend_cslotnorm_pl_kernel(tc, tab_words, tab_scales, w1, gain, wo, dy,
         nc.vector.tensor_copy(dealt(w1_grouped)[:, 80:128, :, :], w1_view[:, 80:128, :, :])
         picked_scales = sbuf("picked_scales", [P, J], U8)
         nc.vector.tensor_copy(picked_scales[:], table_scales[:].indirect(offsets[:]))
-        w1_codes, w1_scales = quantise("w1", w1_grouped, R)
+        w1_codes, w1_scales = quantise("w1", w1_grouped[:], R)
         picked_words = []
         for u in range(2):
             picked_words.append(sbuf(f"picked_words{u}", [P, HALF], U32))
@@ -94,33 +99,34 @@ def tile_attend_cslotnorm_pl_kernel(tc, tab_words, tab_scales, w1, gain, wo, dy,
 
         neg_silu = [sbuf(f"neg_silu{t}", [P, J], F32) for t in range(PACK)]
         neg_tanh = [sbuf(f"neg_tanh{t}", [P, J], F32) for t in range(PACK)]
-        mean_sq = sbuf("mean_sq", [P, PACK], F32)
-        for t in range(PACK):
-            nc.scalar.activation(neg_silu[t][:], a_bank[t][:], ACT.Square, scale=root_inv_j[:],
-                                 accum_out=mean_sq[:, t : t + 1])
-        norm = sbuf("norm", [P, PACK], F32)
-        nc.scalar.activation(norm[:], mean_sq[:], ACT.Sqrt, bias=EPS)
+        sum_sq = sbuf("sum_sq", [P, PACK], F32)
+        norm_sq = sbuf("norm_sq", [P, PACK], F32)
+        inv_norm = sbuf("inv_norm", [P, PACK], F32)
+        for u in range(2):
+            for t in (2 * u, 2 * u + 1):
+                nc.scalar.activation(neg_silu[t][:], a_bank[t][:], ACT.Square, bias=zero_bias[:],
+                                     accum_out=sum_sq[:, t : t + 1])
+            nc.scalar.activation(norm_sq[:, 2 * u : 2 * u + 2], sum_sq[:, 2 * u : 2 * u + 2], ACT.Identity, scale=1.0 / J, bias=EPS)
+            nc.gpsimd.tensor_tensor(inv_norm[:, 2 * u : 2 * u + 2], norm_sq[:, 2 * u : 2 * u + 2], minus_half[:], ALU.pow)
 
         wo_grouped = sbuf("wo_grouped", [P, PACK * R], BF16)
-        nc.vector.tensor_copy(wo_grouped[:].rearrange("p (t m i) -> p m i t", t=PACK, i=PACK),
-                              wo_raw[:].rearrange("p i (m t) -> p m i t", t=PACK))
-        wo_codes, wo_scales = quantise("wo", wo_grouped, R)
+        nc.vector.tensor_copy(dealt(wo_grouped), wo_raw[:].rearrange("p i (m t) -> p m i t", t=PACK))
+        wo_codes, wo_scales = quantise("wo", wo_grouped[:], R)
         dy_grouped = [sbuf(f"dy_grouped{u}", [P, PACK * HALF], BF16) for u in range(2)]
-        for u in range(2):
-            nc.vector.tensor_copy(dy_grouped[u][:].rearrange("p (c e i) -> p c i e", e=4, i=PACK),
-                                  dy_raw[:, :, u * HALF : (u + 1) * HALF].rearrange("p i (c e) -> p c i e", e=4))
-        inv_norm = dy_raw[:, 0, HALF : HALF + PACK]
-        nc.vector.reciprocal(inv_norm, norm[:])
-        dy_quant = [quantise("dy0", dy_grouped[0], HALF)]
-        neg_g = sbuf("neg_g", [P, PACK], F32)
-        neg_half_g = sbuf("neg_half_g", [P, PACK], F32)
-        inv_sq = sbuf("inv_sq", [P, PACK], F32)
-        coef = sbuf("coef", [P, PACK], F32)
-        nc.vector.scalar_tensor_tensor(neg_g[:], inv_norm, -1.0, gain_cols[:], ALU.mult, ALU.mult)
-        nc.vector.scalar_tensor_tensor(neg_half_g[:], inv_norm, -0.5, gain_cols[:], ALU.mult, ALU.mult)
-        dy_quant.append(quantise("dy1", dy_grouped[1], HALF))
-        nc.vector.scalar_tensor_tensor(inv_sq[:], inv_norm, 1.0 / J, inv_norm, ALU.mult, ALU.mult)
-        nc.vector.tensor_tensor(coef[:], inv_sq[:], neg_half_g[:], ALU.mult)
+        dy_view = dy_raw[:].rearrange("p i (c e) -> p c i e", e=4)
+
+        def dy_words(u):
+            return dy_grouped[u][:].rearrange("p (c e i) -> p c i e", e=4, i=PACK)
+
+        nc.vector.tensor_copy(dy_words(0), dy_view[:, 0:64, :, :])
+        nc.vector.tensor_copy(dy_words(1)[:, 0:24, :, :], dy_view[:, 64:88, :, :])
+        nc.scalar.copy(dy_words(1)[:, 24:64, :, :], dy_view[:, 88:128, :, :])
+        dy_quant = [quantise(f"dy{u}", dy_grouped[u][:], HALF) for u in range(2)]
+        factors = dy_raw[:, 0, J - 8 : J - 2].rearrange("p (e c) -> p e c", e=2)
+        neg_g = [factors[:, t % 2, 1:2] for t in range(PACK)]
+        neg_half_g = [factors[:, t % 2, 2 * (t // 2) : 2 * (t // 2) + 1] for t in range(PACK)]
+        inv_sq = dy_grouped[1][:, 0 : 2 * PACK].bitcast(F32)
+        nc.vector.reciprocal(inv_sq, norm_sq[:])
         c_bank = [psum.tile([P, J], F32, name=f"c{t}") for t in range(PACK)]
         for t in range(PACK):
             for u in range(2):
@@ -145,19 +151,24 @@ def tile_attend_cslotnorm_pl_kernel(tc, tab_words, tab_scales, w1, gain, wo, dy,
         for u in range(2):
             pair = (2 * u, 2 * u + 1)
             for t in pair:
-                nc.scalar.activation(neg_silu[t][:], a_bank[t][:], ACT.Silu, scale=neg_g[:, t : t + 1])
+                nc.scalar.activation(factors[:, t % 2, u : u + 2], neg_gains[:, t, u : u + 2], ACT.Copy, scale=inv_norm[:, t : t + 1])
             for t in pair:
-                nc.scalar.activation(neg_tanh[t][:], a_bank[t][:], ACT.Tanh, scale=neg_half_g[:, t : t + 1])
+                nc.scalar.activation(neg_silu[t][:], a_bank[t][:], ACT.Silu, scale=neg_g[t])
+            for t in pair:
+                nc.scalar.activation(neg_tanh[t][:], a_bank[t][:], ACT.Tanh, scale=neg_half_g[t])
             for t in pair:
                 nc.vector.scalar_tensor_tensor(part[t][:], neg_silu[t][:], -1.0, c_bank[t][:], ALU.add, ALU.mult)
             for t in pair:
                 nc.vector.scalar_tensor_tensor(two_ds[t][:], neg_tanh[t][:], -1.0, part[t][:], ALU.add, ALU.mult)
             if u == 0:
-                nc.vector.scalar_tensor_tensor(inner[0][:], two_ds[0][:], neg_half_g[:, 0:1], old_rows(0),
+                nc.vector.scalar_tensor_tensor(inner[0][:], two_ds[0][:], neg_half_g[0], old_rows(0),
                                                ALU.mult, ALU.subtract)
+        coef = sbuf("coef", [P, PACK], F32)
+        nc.vector.scalar_tensor_tensor(coef[:].rearrange("p (u e) -> p u e", e=2), inv_sq.rearrange("p (u e) -> p u e", e=2),
+                                       1.0 / J, factors[:, :, 0:3:2].rearrange("p e u -> p u e"), ALU.mult, ALU.mult)
         inner[1] = neg_tanh[3]
         for t in range(1, PACK):
-            nc.scalar.activation(neg_silu[t][:], two_ds[t][:], ACT.Copy, scale=neg_half_g[:, t : t + 1])
+            nc.scalar.activation(neg_silu[t][:], two_ds[t][:], ACT.Copy, scale=neg_half_g[t])
             nc.gpsimd.tensor_tensor(inner[t][:], neg_silu[t][:], old_rows(t), ALU.subtract)
 
         def row_sum(t):

from contextlib import ExitStack

import concourse.mybir as mybir

K, R, F, T, J = 512, 512, 512, 2048, 512
FLOPS = 2 * K * R * J + 2 * F * R * J

F32 = mybir.dt.float32
BF16 = mybir.dt.bfloat16
I32 = mybir.dt.int32
U32 = mybir.dt.uint32
U16 = mybir.dt.uint16
U8 = mybir.dt.uint8
FP8X4 = mybir.dt.float8_e4m3fn_x4
ALU = mybir.AluOpType
ACT = mybir.ActivationFunctionType

P = 128
PACK = 4
HALF = 256
EPS = 0.01


def tile_attend_cslotnorm_pl_kernel(tc, tab_words, tab_scales, w1, gain, wo, dy, old, offs, out_0, out_1, out_2):
    nc = tc.nc
    with ExitStack() as ctx:
        keep = ctx.enter_context(tc.tile_pool(name="keep", bufs=1))
        psum = ctx.enter_context(tc.psum_pool(name="psum", bufs=1))

        def sbuf(name, shape, dtype, tag=None):
            return keep.tile(shape, dtype, name=name, tag=tag or name, align_bytes=64)

        offsets = keep.tile([P, J // 16], U16, name="offsets")
        table_scales = sbuf("table_scales", [P, T], U8)
        nc.vector.memset(table_scales[:].bitcast(I32), 0)
        zero = sbuf("zero", [P, 1], F32)
        nc.vector.memset(zero[:], 0.0)
        minus_half = sbuf("minus_half", [P, 2], F32)
        nc.vector.memset(minus_half[:], -0.5)
        zero_bias = sbuf("zero_bias", [P, 1], F32)
        nc.scalar.activation(zero_bias[:], zero[:], ACT.Silu)

        scale_rows = sbuf("scale_rows", [P, T // 4], I32)
        for q in range(4):
            queue = nc.scalar if q % 2 == 0 else nc.sync
            queue.dma_start(out=scale_rows[q:P:32, :], in_=tab_scales[0, q:16:4, :].bitcast(I32))
        for q in range(4):
            rows = slice(32 * q, 32 * q + 4)
            nc.vector.tensor_copy(table_scales[rows, :].bitcast(I32), scale_rows[rows, :])
        w1_raw = sbuf("w1_raw", [P, PACK, R], F32)
        nc.sync.dma_start(out=w1_raw[:], in_=w1.rearrange("(p i) r -> p i r", i=PACK))
        nc.sync.dma_start(offsets[:], offs)
        gain_cols = sbuf("gain_cols", [P, PACK], F32)
        nc.sync.dma_start(out=gain_cols[:], in_=gain.rearrange("(p t) o -> p (t o)", t=PACK))
        neg_gains = sbuf("neg_gains", [P, PACK, 3], F32)
        for column, factor in enumerate((-0.5, -1.0, -0.5)):
            nc.vector.tensor_scalar(neg_gains[:, :, column], gain_cols[:], factor, None, ALU.mult)
        table_words = sbuf("table_words", [P, T], I32)
        nc.sync.dma_start(out=table_words[:], in_=tab_words[0].rearrange("p n t -> p (n t)").bitcast(I32))
        wo_raw = sbuf("wo_raw", [P, PACK, R], F32)
        nc.sync.dma_start(out=wo_raw[:], in_=wo.rearrange("(p i) r -> p i r", i=PACK))
        dy_raw = sbuf("dy_raw", [P, PACK, J], F32)
        nc.sync.dma_start(out=dy_raw[:], in_=dy.rearrange("(p i) j -> p i j", i=PACK))
        old_pair = []
        for u in range(2):
            old_pair.append(sbuf(f"old{u}", [P, 2, J], F32))
            nc.sync.dma_start(out=old_pair[u][:], in_=old.rearrange("(p t) j -> p t j", t=PACK)[:, 2 * u : 2 * u + 2, :])

        def quantise(name, grouped, width):
            codes = sbuf(name + "_codes", [P, width], U32)
            scales = sbuf(name + "_scales", [P, width], U8)
            nc.vector.quantize_mx(out=codes[:].bitcast(FP8X4), scales=scales[:], in_=grouped)
            return codes, scales

        def dealt(grouped):
            return grouped[:].rearrange("p (t m i) -> p m i t", t=PACK, i=PACK)

        w1_grouped = sbuf("w1_grouped", [P, PACK * R], BF16)
        w1_view = w1_raw[:].rearrange("p i (m t) -> p m i t", t=PACK)
        nc.scalar.copy(dealt(w1_grouped)[:, 0:80, :, :], w1_view[:, 0:80, :, :])
        nc.vector.tensor_copy(dealt(w1_grouped)[:, 80:128, :, :], w1_view[:, 80:128, :, :])
        picked_scales = sbuf("picked_scales", [P, J], U8)
        nc.vector.tensor_copy(picked_scales[:], table_scales[:].indirect(offsets[:]))
        w1_codes, w1_scales = quantise("w1", w1_grouped[:], R)
        picked_words = []
        for u in range(2):
            picked_words.append(sbuf(f"picked_words{u}", [P, HALF], U32))
            nc.vector.tensor_copy(picked_words[u][:],
                                  table_words[:].bitcast(U32).indirect(offsets[:, 16 * u : 16 * (u + 1)]))
        a_bank = [psum.tile([P, J], F32, name=f"a{t}") for t in range(PACK)]
        for t in range(PACK):
            for u in range(2):
                cols = slice(u * HALF, (u + 1) * HALF)
                nc.tensor.matmul_mx(out=a_bank[t][:, cols],
                                    lhsT=w1_codes[:, t * P : (t + 1) * P].bitcast(FP8X4),
                                    lhsT_scale=w1_scales[:, t * P : (t + 1) * P],
                                    rhs=picked_words[u][:].bitcast(FP8X4),
                                    rhs_scale=picked_scales[:, cols], start=True, stop=True)

        neg_silu = [sbuf(f"neg_silu{t}", [P, J], F32) for t in range(PACK)]
        neg_tanh = [sbuf(f"neg_tanh{t}", [P, J], F32) for t in range(PACK)]
        sum_sq = sbuf("sum_sq", [P, PACK], F32)
        norm_sq = sbuf("norm_sq", [P, PACK], F32)
        inv_norm = sbuf("inv_norm", [P, PACK], F32)
        for u in range(2):
            for t in (2 * u, 2 * u + 1):
                nc.scalar.activation(neg_silu[t][:], a_bank[t][:], ACT.Square, bias=zero_bias[:],
                                     accum_out=sum_sq[:, t : t + 1])
            nc.scalar.activation(norm_sq[:, 2 * u : 2 * u + 2], sum_sq[:, 2 * u : 2 * u + 2], ACT.Identity, scale=1.0 / J, bias=EPS)
            nc.gpsimd.tensor_tensor(inv_norm[:, 2 * u : 2 * u + 2], norm_sq[:, 2 * u : 2 * u + 2], minus_half[:], ALU.pow)

        wo_grouped = sbuf("wo_grouped", [P, PACK * R], BF16)
        nc.vector.tensor_copy(dealt(wo_grouped), wo_raw[:].rearrange("p i (m t) -> p m i t", t=PACK))
        wo_codes, wo_scales = quantise("wo", wo_grouped[:], R)
        dy_grouped = [sbuf(f"dy_grouped{u}", [P, PACK * HALF], BF16) for u in range(2)]
        dy_view = dy_raw[:].rearrange("p i (c e) -> p c i e", e=4)

        def dy_words(u):
            return dy_grouped[u][:].rearrange("p (c e i) -> p c i e", e=4, i=PACK)

        nc.vector.tensor_copy(dy_words(0), dy_view[:, 0:64, :, :])
        nc.vector.tensor_copy(dy_words(1)[:, 0:24, :, :], dy_view[:, 64:88, :, :])
        nc.scalar.copy(dy_words(1)[:, 24:64, :, :], dy_view[:, 88:128, :, :])
        dy_quant = [quantise(f"dy{u}", dy_grouped[u][:], HALF) for u in range(2)]
        factors = dy_raw[:, 0, J - 8 : J - 2].rearrange("p (e c) -> p e c", e=2)
        neg_g = [factors[:, t % 2, 1:2] for t in range(PACK)]
        neg_half_g = [factors[:, t % 2, 2 * (t // 2) : 2 * (t // 2) + 1] for t in range(PACK)]
        inv_sq = dy_grouped[1][:, 0 : 2 * PACK].bitcast(F32)
        nc.vector.reciprocal(inv_sq, norm_sq[:])
        c_bank = [psum.tile([P, J], F32, name=f"c{t}") for t in range(PACK)]
        for t in range(PACK):
            for u in range(2):
                nc.tensor.matmul_mx(out=c_bank[t][:, u * HALF : (u + 1) * HALF],
                                    lhsT=wo_codes[:, t * P : (t + 1) * P].bitcast(FP8X4),
                                    lhsT_scale=wo_scales[:, t * P : (t + 1) * P],
                                    rhs=dy_quant[u][0][:].bitcast(FP8X4),
                                    rhs_scale=dy_quant[u][1][:], start=True, stop=True)

        part = [sbuf(f"part{t}", [P, J], F32) for t in range(PACK)]
        two_ds = [sbuf(f"two_ds{t}", [P, J], F32) for t in range(PACK)]
        inner = [sbuf(f"inner{t}", [P, J], F32) if t != 1 else None for t in range(PACK)]
        row_coef = [sbuf(f"row_coef{t}", [P, 1], F32) for t in range(PACK)]
        y_pair = [sbuf(f"y{u}", [P, 2, J], F32) for u in range(2)]
        y_grouped = sbuf("y_grouped", [P, PACK * J], BF16)
        y_words = y_grouped[:].rearrange("p (j t) -> p j t", t=PACK)
        out_rows = out_0.rearrange("(p t) j -> p t j", t=PACK)

        def old_rows(t):
            return old_pair[t // 2][:, t % 2, :]

        for u in range(2):
            pair = (2 * u, 2 * u + 1)
            for t in pair:
                nc.scalar.activation(factors[:, t % 2, u : u + 2], neg_gains[:, t, u : u + 2], ACT.Copy, scale=inv_norm[:, t : t + 1])
            for t in pair:
                nc.scalar.activation(neg_silu[t][:], a_bank[t][:], ACT.Silu, scale=neg_g[t])
            for t in pair:
                nc.scalar.activation(neg_tanh[t][:], a_bank[t][:], ACT.Tanh, scale=neg_half_g[t])
            for t in pair:
                nc.vector.scalar_tensor_tensor(part[t][:], neg_silu[t][:], -1.0, c_bank[t][:], ALU.add, ALU.mult)
            for t in pair:
                nc.vector.scalar_tensor_tensor(two_ds[t][:], neg_tanh[t][:], -1.0, part[t][:], ALU.add, ALU.mult)
            if u == 0:
                nc.vector.scalar_tensor_tensor(inner[0][:], two_ds[0][:], neg_half_g[0], old_rows(0),
                                               ALU.mult, ALU.subtract)
        coef = sbuf("coef", [P, PACK], F32)
        nc.vector.scalar_tensor_tensor(coef[:].rearrange("p (u e) -> p u e", e=2), inv_sq.rearrange("p (u e) -> p u e", e=2),
                                       1.0 / J, factors[:, :, 0:3:2].rearrange("p e u -> p u e"), ALU.mult, ALU.mult)
        inner[1] = neg_tanh[3]
        for t in range(1, PACK):
            nc.scalar.activation(neg_silu[t][:], two_ds[t][:], ACT.Copy, scale=neg_half_g[t])
            nc.gpsimd.tensor_tensor(inner[t][:], neg_silu[t][:], old_rows(t), ALU.subtract)

        def row_sum(t):
            nc.vector.scalar_tensor_tensor(part[t][:], two_ds[t][:], coef[:, t : t + 1], a_bank[t][:],
                                           ALU.mult, ALU.mult, accum_out=row_coef[t][:])

        def result(t, cols):
            nc.vector.scalar_tensor_tensor(y_pair[t // 2][:, t % 2, cols], a_bank[t][:, cols], row_coef[t][:],
                                           inner[t][:, cols], ALU.mult, ALU.subtract)

        def store(t):
            nc.sync.dma_start(out=out_rows[:, t, :], in_=y_pair[t // 2][:, t % 2, :])

        for t in (0, 1):
            row_sum(t)
        for t in (0, 1):
            result(t, slice(0, J))
            store(t)
        nc.scalar.copy(y_words[:, :, 0:2], y_pair[0][:].rearrange("p e j -> p j e"))
        for t in (2, 3):
            row_sum(t)
        y_turned = y_pair[1][:].rearrange("p e j -> p j e")
        for t in (2, 3):
            result(t, slice(0, HALF))
        nc.scalar.copy(y_words[:, 0:HALF, 2:4], y_turned[:, 0:HALF, :])
        for t in (2, 3):
            result(t, slice(HALF, J))
            store(t)
        nc.vector.tensor_copy(y_words[:, HALF:J, 2:4], y_turned[:, HALF:J, :])

        y_codes = sbuf("y_codes", [P, J], U32)
        y_scales = sbuf("y_scales", [P, J], U8)
        out_words = out_1[0].rearrange("p n t -> p (n t)").bitcast(I32)
        for u in range(2):
            cols = slice(u * HALF, (u + 1) * HALF)
            nc.vector.quantize_mx(out=y_codes[:, cols].bitcast(FP8X4), scales=y_scales[:, cols],
                                  in_=y_grouped[:, PACK * HALF * u : PACK * HALF * (u + 1)])
            nc.sync.dma_start(out=out_words[:, cols], in_=y_codes[:, cols].bitcast(I32))
        for q in range(4):
            queue = nc.scalar if q % 2 == 0 else nc.sync
            queue.dma_start(out=out_2[0, q:16:4, :].bitcast(I32), in_=y_scales[q:P:32, :].bitcast(I32))
